import numpy as np
import ml_dtypes


def mxq(x, axis, fmt="e4m3"):
    dtype, down = {"e4m3": (ml_dtypes.float8_e4m3fn, 7), "e5m2": (ml_dtypes.float8_e5m2, 14)}[fmt]
    v = np.moveaxis(np.asarray(x, np.float32).astype(ml_dtypes.bfloat16).astype(np.float64), axis, -1)
    blocks = v.reshape(v.shape[:-1] + (-1, 32))
    amax = np.abs(blocks).max(-1, keepdims=True)
    byte = np.maximum(np.where(amax > 0, np.frexp(amax)[1] - 1 + 127, 0) - down, 1)
    scale = np.exp2(byte - 127.0)
    codes = (blocks / scale).astype(np.float32).astype(dtype).astype(np.float64)
    return np.moveaxis((codes * scale).reshape(v.shape), -1, axis)


WIDE = False


def mx_kscale(k):
    if not WIDE:
        return np.ones(k)
    levels = np.array([10, -10, 5, -5, 0])
    if k % 512:
        return np.exp2(np.random.permutation(np.resize(levels, k // 32))).repeat(32)
    a = np.empty((k // 512, 16))
    for p in range(k // 512):
        a[p, :8] = np.random.permutation(np.resize(levels, 8))
        for g in range(8):
            far = levels[np.abs(levels - a[p, g]) >= 10]
            a[p, g + 8] = far[np.random.randint(len(far))]
    return np.exp2(a.ravel()).repeat(32)


def f64(x):
    return np.asarray(x).astype(np.float64)


def striped(idx):
    return np.tile(idx.reshape(-1, 16).T, (8, 1)).astype(np.uint16)


def unstriped(offs):
    return offs[:16].T.reshape(-1).astype(np.int64)


def striped8(idx):
    return np.concatenate([x.reshape(-1, 16).T for x in idx]).astype(np.uint16)


def runs(offs, k):
    lists = np.stack([offs[16 * r : 16 * r + 16].T.reshape(-1) for r in range(8)]).astype(np.int64)
    return lists[np.arange(k) % 512 // 64]


def pack_weight(w):
    k, n = w.shape
    w = f64(np.asarray(w, np.float32).astype(ml_dtypes.bfloat16)).reshape(k // 32, 32, n)
    amax = np.abs(w).max(1)
    byte = np.clip(np.where(amax > 0, np.frexp(amax)[1] - 1 + 127 - 7, 1), 1, 254)
    scaled = (w * np.exp2(127.0 - byte)[:, None, :]).reshape(k, n).astype(np.float32)
    words = np.ascontiguousarray(scaled.reshape(k // 512, 128, 4, n).transpose(0, 1, 3, 2)).astype(ml_dtypes.float8_e4m3fn).view(np.uint8)
    return words, np.ascontiguousarray(byte.astype(np.uint8).reshape(k // 512, 16, n))


def unpack_weight(words, scales):
    g, p, n, _ = words.shape
    vals = np.ascontiguousarray(words).view(ml_dtypes.float8_e4m3fn).astype(np.float64) * np.repeat(np.exp2(scales.astype(np.float64) - 127.0), 8, axis=1)[..., None]
    return vals.transpose(0, 1, 3, 2).reshape(g * 512, n)


def sigmoid(v):
    return 1.0 / (1.0 + np.exp(-np.maximum(v, -700.0)))


K, T, S, H, C, G, W = 512, 1024, 512, 512, 512, 2048, 256


def setup_inputs():
    n = np.random.standard_normal
    s = mx_kscale(K)[:, None]
    packed_xT = pack_weight(n((K, T)) * s)
    packed_dT = pack_weight(n((K, G)) / s)
    return {
        "x_words": packed_xT[0],
        "x_scales": packed_xT[1],
        "w1": (n((K, H)) / np.sqrt(K) / s).astype(np.float32),
        "gs": (np.random.uniform(0.5, 1.5, (K, 1)) / s).astype(np.float32),
        "gk": (np.random.uniform(0.5, 1.5, (K, 1)) * s).astype(np.float32),
        "d_words": packed_dT[0],
        "d_scales": packed_dT[1],
        "offs": striped(np.random.permutation(T)[:S]),
        "n1": striped8(np.stack([np.random.permutation(S) for _ in range(8)])),
        "n2": striped8(np.stack([np.random.permutation(S) for _ in range(8)])),
        "n3": striped(np.random.permutation(S)),
        "n4": striped(np.random.permutation(S)),
        "cand": striped(np.random.permutation(T)[:C]),
        "k1": striped8(np.random.randint(0, G, (8, H))),
        "n5": striped8(np.stack([np.random.permutation(S)[:W] for _ in range(8)])),
        "n6": striped8(np.stack([np.random.permutation(S)[:W] for _ in range(8)])),
    }


def reference(x_words, x_scales, w1, gs, gk, d_words, d_scales, offs, n1, n2, n3, n4, cand, k1, n5, n6):
    d_k1 = unpack_weight(d_words, d_scales)[np.arange(K)[:, None], runs(k1, K)]
    xq = unpack_weight(x_words, x_scales)[:, unstriped(offs)]
    y = mxq(f64(w1), 0, "e4m3").T @ xq
    st = y - y[:, unstriped(n3)]
    z2 = f64(gk) * (st / (np.abs(st[:, unstriped(n4)]) + 0.5))
    b = 0.0625 * ((d_k1.T @ mxq(z2, 0, "e4m3")))
    x_cand = unpack_weight(x_words, x_scales)[:, unstriped(cand)]
    z = f64(gs) * (np.maximum(y * (sigmoid(y[np.arange(H)[:, None], runs(n1, H)])), y[np.arange(H)[:, None], runs(n2, H)]))
    a = 0.0625 * ((x_cand.T @ mxq(z, 0, "e4m3")))
    ra = b[np.arange(H)[:, None], runs(n6, H)] - (0.5 * (a[np.arange(C)[:, None], runs(n5, C)]))
    out = a.copy()
    out[np.arange(H)[:, None], runs(n5, H)] = ra
    return out

@@ -1,0 +1,208 @@
+from contextlib import ExitStack
+
+import concourse.mybir as mybir
+
+K, T, S, G, W = 512, 1024, 512, 2048, 256
+FLOPS = 3 * 2 * 512 * 512 * 512
+
+F32 = mybir.dt.float32
+BF16 = mybir.dt.bfloat16
+I32 = mybir.dt.int32
+U32 = mybir.dt.uint32
+U16 = mybir.dt.uint16
+U8 = mybir.dt.uint8
+FP8X4 = mybir.dt.float8_e4m3fn_x4
+ALU = mybir.AluOpType
+ACT = mybir.ActivationFunctionType
+
+P = 128
+PACK = 4
+
+
+def tile_picked_cdkeyputbgmaxhopn_none_p_kernel(
+    tc, x_words, x_scales, w1, gs, gk, d_words, d_scales, offs, n1, n2, n3, n4, cand, k1, n5, n6, out
+):
+    nc = tc.nc
+    with ExitStack() as ctx:
+        sb = ctx.enter_context(tc.tile_pool(name="sb", bufs=1))
+        ps = ctx.enter_context(tc.psum_pool(name="ps", bufs=1))
+
+        def sbuf(name, shape, dtype):
+            return sb.tile(shape, dtype, name=name, align_bytes=64)
+
+        def load_list(name, src):
+            tile = sbuf(name, list(src.shape), U16)
+            nc.sync.dma_start(tile[:], src)
+            return tile
+
+        def halves(list_tile):
+            return [(slice(h * (S // 2), (h + 1) * (S // 2)), list_tile[:, h * 16 : (h + 1) * 16]) for h in range(2)]
+
+        x_byte_table = sbuf("x_byte_table", [P, T], U8)
+        nc.vector.memset(x_byte_table[:].bitcast(I32), 0)
+        d_byte_table = sbuf("d_byte_table", [P, G], U8)
+        nc.gpsimd.memset(d_byte_table[:].bitcast(I32), 0)
+        key_bytes = sbuf("key_bytes", [P, S], U8)
+        nc.gpsimd.memset(key_bytes[:].bitcast(I32), 0)
+
+        offs_t = load_list("offs_t", offs)
+        x_word_table = sbuf("x_word_table", [P, T], U32)
+        nc.sync.dma_start(x_word_table[:].bitcast(I32), x_words[0].rearrange("p n t -> p (n t)").bitcast(I32))
+        for r in range(4):
+            nc.scalar.dma_start(x_byte_table[r:P:32, :].bitcast(I32), x_scales[0][r:16:4, :].bitcast(I32))
+        w_rows = w1.rearrange("(p j) c -> p j c", j=PACK)
+        w_raw = []
+        for h in range(2):
+            raw = sbuf(f"w_raw{h}", [P, PACK, 256], F32)
+            nc.sync.dma_start(raw[:], w_rows[:, :, h * 256 : (h + 1) * 256])
+            w_raw.append(raw)
+        n1_t = load_list("n1_t", n1)
+        n3_t = load_list("n3_t", n3)
+        cand_t = load_list("cand_t", cand)
+        k1_t = load_list("k1_t", k1)
+        d_word_table = sbuf("d_word_table", [P, G], U32)
+        nc.sync.dma_start(d_word_table[:].bitcast(I32), d_words[0].rearrange("p n t -> p (n t)").bitcast(I32))
+        for e in range(2):
+            nc.sync.dma_start(d_byte_table[e:P:16, :].bitcast(I32), d_scales[0][e:16:2, :].bitcast(I32))
+        gk_t = sbuf("gk_t", [P, PACK], F32)
+        nc.sync.dma_start(gk_t[:], gk.rearrange("(p t) o -> p (t o)", t=PACK))
+        gs_t = sbuf("gs_t", [P, PACK], F32)
+        nc.sync.dma_start(gs_t[:], gs.rearrange("(p t) o -> p (t o)", t=PACK))
+        n4_t = load_list("n4_t", n4)
+        n2_t = load_list("n2_t", n2)
+        n6_t = load_list("n6_t", n6)
+        n5_t = load_list("n5_t", n5)
+
+        xq_words = sbuf("xq_words", [P, S], U32)
+        nc.vector.tensor_copy(xq_words[:], x_word_table[:].indirect(offs_t[:]))
+        xq_bytes = sbuf("xq_bytes", [P, S], U8)
+        nc.vector.tensor_copy(xq_bytes[:], x_byte_table[:].indirect(offs_t[:]))
+
+        w_bf = sbuf("w_bf", [P, PACK * 512], BF16)
+        w_view = w_bf[:].rearrange("p (t m j) -> p m j t", t=PACK, j=PACK)
+        nc.scalar.copy(w_view[:, 0:64], w_raw[0][:].rearrange("p j (m t) -> p m j t", t=PACK))
+        nc.vector.tensor_copy(w_view[:, 64:128], w_raw[1][:].rearrange("p j (m t) -> p m j t", t=PACK))
+        w_words = sbuf("w_words", [P, 512], U32)
+        w_bytes = sbuf("w_bytes", [P, 512], U8)
+        y_ps = []
+        for t in range(PACK):
+            cols = slice(t * P, (t + 1) * P)
+            nc.vector.quantize_mx(w_words[:, cols].bitcast(FP8X4), w_bytes[:, cols], w_bf[:, t * 512 : (t + 1) * 512])
+            bank = ps.tile([P, S], F32, name=f"ya_bank{t}")
+            nc.tensor.matmul_mx(
+                bank[:], lhsT=w_words[:, cols].bitcast(FP8X4), lhsT_scale=w_bytes[:, cols],
+                rhs=xq_words[:].bitcast(FP8X4), rhs_scale=xq_bytes[:], start=True, stop=True,
+            )
+            y_ps.append(bank)
+
+        y = [sbuf(f"y{t}", [P, S], F32) for t in range(PACK)]
+        sig = [sbuf(f"sig{t}", [P, S], F32) for t in range(PACK)]
+        y3 = [sbuf(f"y3_{t}", [P, S], F32) for t in range(PACK)]
+        st = sbuf("st", [P, PACK, S], F32)
+        for t in range(PACK):
+            if t == 0:
+                nc.vector.tensor_copy(y[t][:], y_ps[t][:])
+            else:
+                nc.scalar.copy(y[t][:], y_ps[t][:])
+            for cols, piece in halves(n1_t):
+                nc.scalar.activation(sig[t][:, cols], y[t][:].indirect(piece), ACT.Sigmoid)
+            for cols, piece in halves(n3_t):
+                nc.vector.tensor_copy(y3[t][:, cols], y[t][:].indirect(piece))
+            nc.vector.tensor_tensor(st[:, t, :], y[t][:], y3[t][:], ALU.subtract)
+
+        mag = [sbuf(f"mag{t}", [P, S], F32) for t in range(PACK)]
+        root = [sbuf(f"root{t}", [P, S], F32) for t in range(PACK)]
+        recip = [sbuf(f"recip{t}", [P, S], F32) for t in range(PACK)]
+        recip4 = sbuf("recip4", [P, PACK, S], F32)
+        for t in range(PACK):
+            nc.vector.scalar_tensor_tensor(mag[t][:], st[:, t, :], -1.0, st[:, t, :], ALU.mult, ALU.max)
+            nc.scalar.activation(root[t][:], mag[t][:], ACT.Abs_reciprocal_sqrt, bias=0.5)
+        for t in range(PACK):
+            nc.vector.scalar_tensor_tensor(recip[t][:], root[t][:], gk_t[:, t : t + 1], root[t][:], ALU.mult, ALU.mult)
+            for cols, piece in halves(n4_t):
+                nc.scalar.activation(recip4[:, t, cols], recip[t][:].indirect(piece), ACT.Copy)
+
+        def deal(name, src, dtype):
+            dealt = sbuf(name, [P, S], dtype)
+            nc.vector.tensor_copy(
+                dealt[:].rearrange("p (t m) -> p m t", t=PACK), src[:].rearrange("p (m t) -> p m t", t=PACK)
+            )
+            return dealt
+
+        kg_words = sbuf("kg_words", [P, S], U32)
+        kg_bytes = sbuf("kg_bytes", [P, S], U8)
+        nc.vector.tensor_copy(kg_bytes[:], d_byte_table[:].indirect(k1_t[:]))
+        nc.vector.tensor_copy(kg_words[:], d_word_table[:].indirect(k1_t[:]))
+        kd_bytes = deal("kd_bytes", kg_bytes, U8)
+        for r in range(4):
+            first = 16 * (r // 2) + r % 2
+            nc.sync.dma_start(key_bytes[r:P:32, :].bitcast(I32), kd_bytes[first:P:32, :].bitcast(I32))
+        key_words = deal("key_words", kg_words, U32)
+
+        gated = [sbuf(f"gated{t}", [P, S], F32) for t in range(PACK)]
+        for t in range(PACK):
+            nc.vector.tensor_tensor(gated[t][:], y[t][:], sig[t][:], ALU.mult)
+
+        def interleaved(planes):
+            return planes.rearrange("p t (c i) -> p c t i", i=4)
+
+        def product(name, bf, words, scale_bytes, tag):
+            q_words = sbuf(name + "_words", [P, S], U32)
+            q_bytes = sbuf(name + "_bytes", [P, S], U8)
+            nc.vector.quantize_mx(q_words[:].bitcast(FP8X4), q_bytes[:], bf[:])
+            banks = []
+            for t in range(PACK):
+                cols = slice(t * P, (t + 1) * P)
+                bank = ps.tile([P, S], F32, name=f"{tag}{t}")
+                nc.tensor.matmul_mx(
+                    bank[:], lhsT=words[:, cols].bitcast(FP8X4), lhsT_scale=scale_bytes[:, cols],
+                    rhs=q_words[:].bitcast(FP8X4), rhs_scale=q_bytes[:], start=True, stop=True,
+                )
+                banks.append(bank)
+            return banks
+
+        z2_bf = sbuf("z2_bf", [P, S * PACK], BF16)
+        nc.vector.tensor_tensor(
+            z2_bf[:].rearrange("p (c i t) -> p c t i", i=4, t=PACK), interleaved(recip4[:]), interleaved(st[:]), ALU.mult
+        )
+        b_ps = product("z2", z2_bf, key_words, key_bytes, "b_bank")
+
+        y2 = [sbuf(f"y2_{t}", [P, S], F32) for t in range(PACK)]
+        larger = sbuf("larger", [P, PACK, S], F32)
+        for t in range(PACK):
+            for cols, piece in halves(n2_t):
+                nc.scalar.activation(y2[t][:, cols], y[t][:].indirect(piece), ACT.Copy)
+            nc.vector.tensor_tensor(larger[:, t, :], gated[t][:], y2[t][:], ALU.max)
+
+        cg_words = sbuf("cg_words", [P, S], U32)
+        cg_bytes = sbuf("cg_bytes", [P, S], U8)
+        nc.vector.tensor_copy(cg_words[:], x_word_table[:].indirect(cand_t[:]))
+        nc.vector.tensor_copy(cg_bytes[:], x_byte_table[:].indirect(cand_t[:]))
+        cand_words = deal("cand_words", cg_words, U32)
+        cand_bytes = deal("cand_bytes", cg_bytes, U8)
+
+        z_bf = sbuf("z_bf", [P, S * PACK], BF16)
+        nc.vector.tensor_tensor(
+            z_bf[:].rearrange("p (c i t) -> p c t i", i=4, t=PACK),
+            interleaved(larger[:]),
+            gs_t[:].unsqueeze(1).unsqueeze(3).to_broadcast([P, S // 4, PACK, 4]),
+            ALU.mult,
+        )
+        a_ps = product("z", z_bf, cand_words, cand_bytes, "ya_bank")
+
+        b6 = []
+        for t in range(PACK):
+            b_sb = sbuf(f"b{t}", [P, S], F32)
+            nc.scalar.activation(b_sb[:], b_ps[t][:], ACT.Copy, scale=0.0625)
+            picked = sbuf(f"b6_{t}", [P, W], F32)
+            nc.scalar.activation(picked[:], b_sb[:].indirect(n6_t[:]), ACT.Copy)
+            b6.append(picked)
+
+        out_rows = out.rearrange("(p t) n -> p t n", t=PACK)
+        for t in range(PACK):
+            a_sb = sbuf(f"a{t}", [P, S], F32)
+            nc.scalar.activation(a_sb[:], a_ps[t][:], ACT.Copy, scale=0.0625)
+            a5 = sbuf(f"a5_{t}", [P, W], F32)
+            nc.scalar.activation(a5[:], a_sb[:].indirect(n5_t[:]), ACT.Copy, scale=-0.5)
+            nc.vector.tensor_tensor(a_sb[:].indirect(n5_t[:]), b6[t][:], a5[:], ALU.add)
+            nc.sync.dma_start(out_rows[:, t, :], a_sb[:])

@@ -2,7 +2,7 @@ from contextlib import ExitStack
 
 import concourse.mybir as mybir
 
-K, T, S, G, W = 512, 1024, 512, 2048, 256
+T, S, G, W = 1024, 512, 2048, 256
 FLOPS = 3 * 2 * 512 * 512 * 512
 
 F32 = mybir.dt.float32
@@ -17,6 +17,11 @@ ACT = mybir.ActivationFunctionType
 
 P = 128
 PACK = 4
+RUN = 8
+LINE = 4
+HALF = P // 2
+W_SPLIT = 96
+SCORE_SCALE = 0.0625
 
 
 def tile_picked_cdkeyputbgmaxhopn_none_p_kernel(
@@ -26,183 +31,201 @@ def tile_picked_cdkeyputbgmaxhopn_none_p_kernel(
     with ExitStack() as ctx:
         sb = ctx.enter_context(tc.tile_pool(name="sb", bufs=1))
         ps = ctx.enter_context(tc.psum_pool(name="ps", bufs=1))
+        four = range(PACK)
 
         def sbuf(name, shape, dtype):
             return sb.tile(shape, dtype, name=name, align_bytes=64)
+
+        def four_tiles(name, columns):
+            return [sbuf(f"{name}{t}", [P, columns], F32) for t in four]
 
         def load_list(name, src):
             tile = sbuf(name, list(src.shape), U16)
             nc.sync.dma_start(tile[:], src)
             return tile
 
-        def halves(list_tile):
-            return [(slice(h * (S // 2), (h + 1) * (S // 2)), list_tile[:, h * 16 : (h + 1) * 16]) for h in range(2)]
+        def load_words(name, src, columns):
+            tile = sbuf(name, [P, columns], U32)
+            nc.sync.dma_start(tile[:].bitcast(I32), src[0].rearrange("p n t -> p (n t)").bitcast(I32))
+            return tile
 
-        x_byte_table = sbuf("x_byte_table", [P, T], U8)
-        nc.vector.memset(x_byte_table[:].bitcast(I32), 0)
-        d_byte_table = sbuf("d_byte_table", [P, G], U8)
-        nc.gpsimd.memset(d_byte_table[:].bitcast(I32), 0)
-        key_bytes = sbuf("key_bytes", [P, S], U8)
-        nc.gpsimd.memset(key_bytes[:].bitcast(I32), 0)
+        def load_feature_weights(name, src):
+            tile = sbuf(name, [P, PACK], F32)
+            nc.sync.dma_start(tile[:], src.rearrange("(p t) o -> p (t o)", t=PACK))
+            return tile
+
+        def zeroed_bytes(name, columns):
+            tile = sbuf(name, [P, columns], U8)
+            nc.gpsimd.memset(tile[:].bitcast(I32), 0)
+            return tile
+
+        def pick(name, table, list_tile, dtype):
+            picked = sbuf(name, [P, S], dtype)
+            nc.vector.tensor_copy(picked[:], table[:].indirect(list_tile[:]))
+            return picked
+
+        def deal(dealt, picked):
+            nc.vector.tensor_copy(
+                dealt.rearrange("p (t u e) -> p u t e", t=PACK, u=P // RUN),
+                picked.rearrange("p (u t e) -> p u t e", t=PACK, u=P // RUN),
+            )
+
+        def deal_words(name, picked):
+            dealt = sbuf(name, [P, S], U32)
+            deal(dealt[:], picked[:])
+            return dealt
+
+        def deal_bytes(name, picked):
+            dealt = sbuf(name, [P, S], U8)
+            deal(dealt[:].bitcast(I32), picked[:].bitcast(I32))
+            return dealt
+
+        def gather(on_vector, dst, window, list_tile):
+            if on_vector:
+                nc.vector.tensor_copy(dst, window[:].indirect(list_tile[:]))
+            else:
+                nc.scalar.activation(dst, window[:].indirect(list_tile[:]), ACT.Copy)
+
+        def multiply(bank_name, t, words, scale_bytes, moving_words, moving_bytes):
+            cols = slice(t * P, (t + 1) * P)
+            bank = ps.tile([P, S], F32, name=f"{bank_name}{t}")
+            nc.tensor.matmul_mx(
+                bank[:],
+                lhsT=words[:, cols].bitcast(FP8X4),
+                lhsT_scale=scale_bytes[:, cols],
+                rhs=moving_words[:].bitcast(FP8X4),
+                rhs_scale=moving_bytes[:],
+                start=True,
+                stop=True,
+            )
+            return bank
+
+        def by_lines(planes):
+            return planes[:].rearrange("p t (c i) -> p c t i", i=LINE)
+
+        def score(name, factor0, factor1, words, scale_bytes, bank_name):
+            rounded = sbuf(name + "_bf", [P, S * PACK], BF16)
+            nc.vector.tensor_tensor(
+                rounded[:].rearrange("p (c i t) -> p c t i", i=LINE, t=PACK), factor0, factor1, ALU.mult
+            )
+            q_words = sbuf(name + "_words", [P, S], U32)
+            q_bytes = sbuf(name + "_bytes", [P, S], U8)
+            nc.vector.quantize_mx(q_words[:].bitcast(FP8X4), q_bytes[:], rounded[:])
+            return [multiply(bank_name, t, words, scale_bytes, q_words, q_bytes) for t in four]
+
+        x_byte_table = zeroed_bytes("x_byte_table", T)
+        warm = sbuf("warm", [P, 2], F32)
+        nc.gpsimd.memset(warm[:, 0:1], 0.0)
+        nc.scalar.activation(warm[:, 1:2], warm[:, 0:1], ACT.Sigmoid)
+        d_byte_table = zeroed_bytes("d_byte_table", G)
+        key_bytes = zeroed_bytes("key_bytes", S)
 
         offs_t = load_list("offs_t", offs)
-        x_word_table = sbuf("x_word_table", [P, T], U32)
-        nc.sync.dma_start(x_word_table[:].bitcast(I32), x_words[0].rearrange("p n t -> p (n t)").bitcast(I32))
-        for r in range(4):
-            nc.scalar.dma_start(x_byte_table[r:P:32, :].bitcast(I32), x_scales[0][r:16:4, :].bitcast(I32))
+        x_word_table = load_words("x_word_table", x_words, T)
+        for r in four:
+            nc.sync.dma_start(x_byte_table[r:P:32, :].bitcast(I32), x_scales[0][r:16:4, :].bitcast(I32))
         w_rows = w1.rearrange("(p j) c -> p j c", j=PACK)
         w_raw = []
         for h in range(2):
-            raw = sbuf(f"w_raw{h}", [P, PACK, 256], F32)
-            nc.sync.dma_start(raw[:], w_rows[:, :, h * 256 : (h + 1) * 256])
-            w_raw.append(raw)
+            raw = sbuf(f"w_raw{h}", [P, PACK, PACK * HALF], F32)
+            nc.sync.dma_start(raw[:], w_rows[:, :, h * PACK * HALF : (h + 1) * PACK * HALF])
+            w_raw.append(raw[:].rearrange("p j (m t) -> p m j t", t=PACK))
         n1_t = load_list("n1_t", n1)
         n3_t = load_list("n3_t", n3)
         cand_t = load_list("cand_t", cand)
-        k1_t = load_list("k1_t", k1)
-        d_word_table = sbuf("d_word_table", [P, G], U32)
-        nc.sync.dma_start(d_word_table[:].bitcast(I32), d_words[0].rearrange("p n t -> p (n t)").bitcast(I32))
+        n2_t = load_list("n2_t", n2)
         for e in range(2):
             nc.sync.dma_start(d_byte_table[e:P:16, :].bitcast(I32), d_scales[0][e:16:2, :].bitcast(I32))
-        gk_t = sbuf("gk_t", [P, PACK], F32)
-        nc.sync.dma_start(gk_t[:], gk.rearrange("(p t) o -> p (t o)", t=PACK))
-        gs_t = sbuf("gs_t", [P, PACK], F32)
-        nc.sync.dma_start(gs_t[:], gs.rearrange("(p t) o -> p (t o)", t=PACK))
+        k1_t = load_list("k1_t", k1)
+        d_word_table = load_words("d_word_table", d_words, G)
+        gs_t = load_feature_weights("gs_t", gs)
+        gk_t = load_feature_weights("gk_t", gk)
         n4_t = load_list("n4_t", n4)
-        n2_t = load_list("n2_t", n2)
-        n6_t = load_list("n6_t", n6)
         n5_t = load_list("n5_t", n5)
+        n6_t = load_list("n6_t", n6)
 
-        xq_words = sbuf("xq_words", [P, S], U32)
-        nc.vector.tensor_copy(xq_words[:], x_word_table[:].indirect(offs_t[:]))
-        xq_bytes = sbuf("xq_bytes", [P, S], U8)
-        nc.vector.tensor_copy(xq_bytes[:], x_byte_table[:].indirect(offs_t[:]))
-
-        w_bf = sbuf("w_bf", [P, PACK * 512], BF16)
-        w_view = w_bf[:].rearrange("p (t m j) -> p m j t", t=PACK, j=PACK)
-        nc.scalar.copy(w_view[:, 0:64], w_raw[0][:].rearrange("p j (m t) -> p m j t", t=PACK))
-        nc.vector.tensor_copy(w_view[:, 64:128], w_raw[1][:].rearrange("p j (m t) -> p m j t", t=PACK))
-        w_words = sbuf("w_words", [P, 512], U32)
-        w_bytes = sbuf("w_bytes", [P, 512], U8)
-        y_ps = []
-        for t in range(PACK):
+        xq_words = pick("xq_words", x_word_table, offs_t, U32)
+        xq_bytes = pick("xq_bytes", x_byte_table, offs_t, U8)
+        w_bf = sbuf("w_bf", [P, PACK * S], BF16)
+        w_dealt = w_bf[:].rearrange("p (t m j) -> p m j t", t=PACK, j=PACK)
+        nc.scalar.copy(w_dealt[:, :HALF], w_raw[0])
+        nc.scalar.copy(w_dealt[:, HALF:W_SPLIT], w_raw[1][:, : W_SPLIT - HALF])
+        nc.vector.tensor_copy(w_dealt[:, W_SPLIT:], w_raw[1][:, W_SPLIT - HALF :])
+        w_words = sbuf("w_words", [P, S], U32)
+        w_bytes = sbuf("w_bytes", [P, S], U8)
+        y_banks = []
+        for t in four:
             cols = slice(t * P, (t + 1) * P)
-            nc.vector.quantize_mx(w_words[:, cols].bitcast(FP8X4), w_bytes[:, cols], w_bf[:, t * 512 : (t + 1) * 512])
-            bank = ps.tile([P, S], F32, name=f"ya_bank{t}")
-            nc.tensor.matmul_mx(
-                bank[:], lhsT=w_words[:, cols].bitcast(FP8X4), lhsT_scale=w_bytes[:, cols],
-                rhs=xq_words[:].bitcast(FP8X4), rhs_scale=xq_bytes[:], start=True, stop=True,
-            )
-            y_ps.append(bank)
+            nc.vector.quantize_mx(w_words[:, cols].bitcast(FP8X4), w_bytes[:, cols], w_bf[:, t * S : (t + 1) * S])
+            y_banks.append(multiply("yb_bank", t, w_words, w_bytes, xq_words, xq_bytes))
 
-        y = [sbuf(f"y{t}", [P, S], F32) for t in range(PACK)]
-        sig = [sbuf(f"sig{t}", [P, S], F32) for t in range(PACK)]
-        y3 = [sbuf(f"y3_{t}", [P, S], F32) for t in range(PACK)]
+        y = four_tiles("y", 2 * S)
+        sig1 = four_tiles("sig1_", S)
+        for t in four:
+            nc.scalar.copy(y[t][:, :S], y_banks[t][:])
+            nc.scalar.activation(sig1[t][:], y[t][:].indirect(n1_t[:]), ACT.Sigmoid)
+
+        y3 = four_tiles("y3_", S)
         st = sbuf("st", [P, PACK, S], F32)
-        for t in range(PACK):
-            if t == 0:
-                nc.vector.tensor_copy(y[t][:], y_ps[t][:])
-            else:
-                nc.scalar.copy(y[t][:], y_ps[t][:])
-            for cols, piece in halves(n1_t):
-                nc.scalar.activation(sig[t][:, cols], y[t][:].indirect(piece), ACT.Sigmoid)
-            for cols, piece in halves(n3_t):
-                nc.vector.tensor_copy(y3[t][:, cols], y[t][:].indirect(piece))
-            nc.vector.tensor_tensor(st[:, t, :], y[t][:], y3[t][:], ALU.subtract)
+        for t in four:
+            nc.vector.tensor_copy(y3[t][:], y[t][:].indirect(n3_t[:]))
+            nc.vector.tensor_tensor(st[:, t, :], y[t][:, :S], y3[t][:], ALU.subtract)
 
-        mag = [sbuf(f"mag{t}", [P, S], F32) for t in range(PACK)]
-        root = [sbuf(f"root{t}", [P, S], F32) for t in range(PACK)]
-        recip = [sbuf(f"recip{t}", [P, S], F32) for t in range(PACK)]
-        recip4 = sbuf("recip4", [P, PACK, S], F32)
-        for t in range(PACK):
-            nc.vector.scalar_tensor_tensor(mag[t][:], st[:, t, :], -1.0, st[:, t, :], ALU.mult, ALU.max)
-            nc.scalar.activation(root[t][:], mag[t][:], ACT.Abs_reciprocal_sqrt, bias=0.5)
-        for t in range(PACK):
-            nc.vector.scalar_tensor_tensor(recip[t][:], root[t][:], gk_t[:, t : t + 1], root[t][:], ALU.mult, ALU.mult)
-            for cols, piece in halves(n4_t):
-                nc.scalar.activation(recip4[:, t, cols], recip[t][:].indirect(piece), ACT.Copy)
+        gated = four_tiles("gated", S)
+        for t in four:
+            nc.vector.tensor_tensor(gated[t][:], y[t][:, :S], sig1[t][:], ALU.mult)
+        y2 = four_tiles("y2_", S)
+        for t in four:
+            nc.scalar.activation(y2[t][:], y[t][:].indirect(n2_t[:]), ACT.Copy)
 
-        def deal(name, src, dtype):
-            dealt = sbuf(name, [P, S], dtype)
-            nc.vector.tensor_copy(
-                dealt[:].rearrange("p (t m) -> p m t", t=PACK), src[:].rearrange("p (m t) -> p m t", t=PACK)
-            )
-            return dealt
+        size = four_tiles("size", S)
+        root = four_tiles("root", S)
+        for t in four:
+            nc.scalar.activation(size[t][:], st[:, t, :], ACT.Abs)
+        for t in four:
+            nc.scalar.activation(root[t][:], size[t][:], ACT.Abs_reciprocal_sqrt, bias=0.5)
 
-        kg_words = sbuf("kg_words", [P, S], U32)
-        kg_bytes = sbuf("kg_bytes", [P, S], U8)
-        nc.vector.tensor_copy(kg_bytes[:], d_byte_table[:].indirect(k1_t[:]))
-        nc.vector.tensor_copy(kg_words[:], d_word_table[:].indirect(k1_t[:]))
-        kd_bytes = deal("kd_bytes", kg_bytes, U8)
-        for r in range(4):
-            first = 16 * (r // 2) + r % 2
-            nc.sync.dma_start(key_bytes[r:P:32, :].bitcast(I32), kd_bytes[first:P:32, :].bitcast(I32))
-        key_words = deal("key_words", kg_words, U32)
-
-        gated = [sbuf(f"gated{t}", [P, S], F32) for t in range(PACK)]
-        for t in range(PACK):
-            nc.vector.tensor_tensor(gated[t][:], y[t][:], sig[t][:], ALU.mult)
-
-        def interleaved(planes):
-            return planes.rearrange("p t (c i) -> p c t i", i=4)
-
-        def product(name, bf, words, scale_bytes, tag):
-            q_words = sbuf(name + "_words", [P, S], U32)
-            q_bytes = sbuf(name + "_bytes", [P, S], U8)
-            nc.vector.quantize_mx(q_words[:].bitcast(FP8X4), q_bytes[:], bf[:])
-            banks = []
-            for t in range(PACK):
-                cols = slice(t * P, (t + 1) * P)
-                bank = ps.tile([P, S], F32, name=f"{tag}{t}")
-                nc.tensor.matmul_mx(
-                    bank[:], lhsT=words[:, cols].bitcast(FP8X4), lhsT_scale=scale_bytes[:, cols],
-                    rhs=q_words[:].bitcast(FP8X4), rhs_scale=q_bytes[:], start=True, stop=True,
-                )
-                banks.append(bank)
-            return banks
-
-        z2_bf = sbuf("z2_bf", [P, S * PACK], BF16)
-        nc.vector.tensor_tensor(
-            z2_bf[:].rearrange("p (c i t) -> p c t i", i=4, t=PACK), interleaved(recip4[:]), interleaved(st[:]), ALU.mult
-        )
-        b_ps = product("z2", z2_bf, key_words, key_bytes, "b_bank")
-
-        y2 = [sbuf(f"y2_{t}", [P, S], F32) for t in range(PACK)]
         larger = sbuf("larger", [P, PACK, S], F32)
-        for t in range(PACK):
-            for cols, piece in halves(n2_t):
-                nc.scalar.activation(y2[t][:, cols], y[t][:].indirect(piece), ACT.Copy)
+        for t in four:
             nc.vector.tensor_tensor(larger[:, t, :], gated[t][:], y2[t][:], ALU.max)
 
-        cg_words = sbuf("cg_words", [P, S], U32)
-        cg_bytes = sbuf("cg_bytes", [P, S], U8)
-        nc.vector.tensor_copy(cg_words[:], x_word_table[:].indirect(cand_t[:]))
-        nc.vector.tensor_copy(cg_bytes[:], x_byte_table[:].indirect(cand_t[:]))
-        cand_words = deal("cand_words", cg_words, U32)
-        cand_bytes = deal("cand_bytes", cg_bytes, U8)
+        cand_picked_words = pick("cand_picked_words", x_word_table, cand_t, U32)
+        cand_picked_bytes = pick("cand_picked_bytes", x_byte_table, cand_t, U8)
+        cand_words = deal_words("cand_words", cand_picked_words)
+        cand_bytes = deal_bytes("cand_bytes", cand_picked_bytes)
 
-        z_bf = sbuf("z_bf", [P, S * PACK], BF16)
-        nc.vector.tensor_tensor(
-            z_bf[:].rearrange("p (c i t) -> p c t i", i=4, t=PACK),
-            interleaved(larger[:]),
-            gs_t[:].unsqueeze(1).unsqueeze(3).to_broadcast([P, S // 4, PACK, 4]),
-            ALU.mult,
-        )
-        a_ps = product("z", z_bf, cand_words, cand_bytes, "ya_bank")
+        key_dealt_bytes = deal_bytes("key_dealt_bytes", pick("key_picked_bytes", d_byte_table, k1_t, U8))
+        for r in four:
+            first = 16 * (r // 2) + r % 2
+            nc.sync.dma_start(key_bytes[r:P:32, :].bitcast(I32), key_dealt_bytes[first:P:32, :].bitcast(I32))
 
-        b6 = []
-        for t in range(PACK):
-            b_sb = sbuf(f"b{t}", [P, S], F32)
-            nc.scalar.activation(b_sb[:], b_ps[t][:], ACT.Copy, scale=0.0625)
-            picked = sbuf(f"b6_{t}", [P, W], F32)
-            nc.scalar.activation(picked[:], b_sb[:].indirect(n6_t[:]), ACT.Copy)
-            b6.append(picked)
+        weight = four_tiles("weight", 2 * S)
+        weight4 = sbuf("weight4", [P, PACK, S], F32)
+        for t in four:
+            nc.vector.scalar_tensor_tensor(
+                weight[t][:, :S], root[t][:], gk_t[:, t : t + 1], root[t][:], ALU.mult, ALU.mult
+            )
+            gather(t == PACK - 1, weight4[:, t, :], weight[t], n4_t)
 
-        out_rows = out.rearrange("(p t) n -> p t n", t=PACK)
-        for t in range(PACK):
-            a_sb = sbuf(f"a{t}", [P, S], F32)
-            nc.scalar.activation(a_sb[:], a_ps[t][:], ACT.Copy, scale=0.0625)
-            a5 = sbuf(f"a5_{t}", [P, W], F32)
-            nc.scalar.activation(a5[:], a_sb[:].indirect(n5_t[:]), ACT.Copy, scale=-0.5)
-            nc.vector.tensor_tensor(a_sb[:].indirect(n5_t[:]), b6[t][:], a5[:], ALU.add)
-            nc.sync.dma_start(out_rows[:, t, :], a_sb[:])
+        gs_spread = gs_t[:].unsqueeze(1).unsqueeze(3).to_broadcast([P, S // LINE, PACK, LINE])
+        a_banks = score("z", by_lines(larger), gs_spread, cand_words, cand_bytes, "a_bank")
+        key_words = deal_words("key_words", pick("key_picked_words", d_word_table, k1_t, U32))
+        b_banks = score("z2", by_lines(weight4), by_lines(st), key_words, key_bytes, "yb_bank")
+
+        a = four_tiles("a", S)
+        a5 = four_tiles("a5_", W)
+        for t in four:
+            nc.scalar.activation(a[t][:], a_banks[t][:], ACT.Copy, scale=SCORE_SCALE)
+            nc.scalar.activation(a5[t][:], a[t][:].indirect(n5_t[:]), ACT.Copy, scale=-0.5)
+
+        b = four_tiles("b", S)
+        b6 = four_tiles("b6_", W)
+        out_rows = out.rearrange("(u t e) n -> t u e n", t=PACK, e=RUN)
+        for t in four:
+            if t == 0:
+                nc.vector.tensor_scalar(b[t][:], b_banks[t][:], SCORE_SCALE, None, ALU.mult)
+            else:
+                nc.scalar.activation(b[t][:], b_banks[t][:], ACT.Copy, scale=SCORE_SCALE)
+            gather(t == 0, b6[t][:], b[t], n6_t)
+            nc.vector.tensor_tensor(a[t][:].indirect(n5_t[:]), b6[t][:], a5[t][:], ALU.add)
+            nc.sync.dma_start(out_rows[t], a[t][:])

from contextlib import ExitStack

import concourse.mybir as mybir

T, S, G, W = 1024, 512, 2048, 256
FLOPS = 3 * 2 * 512 * 512 * 512

F32 = mybir.dt.float32
BF16 = mybir.dt.bfloat16
I32 = mybir.dt.int32
U32 = mybir.dt.uint32
U16 = mybir.dt.uint16
U8 = mybir.dt.uint8
FP8X4 = mybir.dt.float8_e4m3fn_x4
ALU = mybir.AluOpType
ACT = mybir.ActivationFunctionType

P = 128
PACK = 4
RUN = 8
LINE = 4
HALF = P // 2
W_SPLIT = 96
SCORE_SCALE = 0.0625


def tile_picked_cdkeyputbgmaxhopn_none_p_kernel(
    tc, x_words, x_scales, w1, gs, gk, d_words, d_scales, offs, n1, n2, n3, n4, cand, k1, n5, n6, out
):
    nc = tc.nc
    with ExitStack() as ctx:
        sb = ctx.enter_context(tc.tile_pool(name="sb", bufs=1))
        ps = ctx.enter_context(tc.psum_pool(name="ps", bufs=1))
        four = range(PACK)

        def sbuf(name, shape, dtype):
            return sb.tile(shape, dtype, name=name, align_bytes=64)

        def four_tiles(name, columns):
            return [sbuf(f"{name}{t}", [P, columns], F32) for t in four]

        def load_list(name, src):
            tile = sbuf(name, list(src.shape), U16)
            nc.sync.dma_start(tile[:], src)
            return tile

        def load_words(name, src, columns):
            tile = sbuf(name, [P, columns], U32)
            nc.sync.dma_start(tile[:].bitcast(I32), src[0].rearrange("p n t -> p (n t)").bitcast(I32))
            return tile

        def load_feature_weights(name, src):
            tile = sbuf(name, [P, PACK], F32)
            nc.sync.dma_start(tile[:], src.rearrange("(p t) o -> p (t o)", t=PACK))
            return tile

        def zeroed_bytes(name, columns):
            tile = sbuf(name, [P, columns], U8)
            nc.gpsimd.memset(tile[:].bitcast(I32), 0)
            return tile

        def pick(name, table, list_tile, dtype):
            picked = sbuf(name, [P, S], dtype)
            nc.vector.tensor_copy(picked[:], table[:].indirect(list_tile[:]))
            return picked

        def deal(dealt, picked):
            nc.vector.tensor_copy(
                dealt.rearrange("p (t u e) -> p u t e", t=PACK, u=P // RUN),
                picked.rearrange("p (u t e) -> p u t e", t=PACK, u=P // RUN),
            )

        def deal_words(name, picked):
            dealt = sbuf(name, [P, S], U32)
            deal(dealt[:], picked[:])
            return dealt

        def deal_bytes(name, picked):
            dealt = sbuf(name, [P, S], U8)
            deal(dealt[:].bitcast(I32), picked[:].bitcast(I32))
            return dealt

        def gather(on_vector, dst, window, list_tile):
            if on_vector:
                nc.vector.tensor_copy(dst, window[:].indirect(list_tile[:]))
            else:
                nc.scalar.activation(dst, window[:].indirect(list_tile[:]), ACT.Copy)

        def multiply(bank_name, t, words, scale_bytes, moving_words, moving_bytes):
            cols = slice(t * P, (t + 1) * P)
            bank = ps.tile([P, S], F32, name=f"{bank_name}{t}")
            nc.tensor.matmul_mx(
                bank[:],
                lhsT=words[:, cols].bitcast(FP8X4),
                lhsT_scale=scale_bytes[:, cols],
                rhs=moving_words[:].bitcast(FP8X4),
                rhs_scale=moving_bytes[:],
                start=True,
                stop=True,
            )
            return bank

        def by_lines(planes):
            return planes[:].rearrange("p t (c i) -> p c t i", i=LINE)

        def score(name, factor0, factor1, words, scale_bytes, bank_name):
            rounded = sbuf(name + "_bf", [P, S * PACK], BF16)
            nc.vector.tensor_tensor(
                rounded[:].rearrange("p (c i t) -> p c t i", i=LINE, t=PACK), factor0, factor1, ALU.mult
            )
            q_words = sbuf(name + "_words", [P, S], U32)
            q_bytes = sbuf(name + "_bytes", [P, S], U8)
            nc.vector.quantize_mx(q_words[:].bitcast(FP8X4), q_bytes[:], rounded[:])
            return [multiply(bank_name, t, words, scale_bytes, q_words, q_bytes) for t in four]

        x_byte_table = zeroed_bytes("x_byte_table", T)
        warm = sbuf("warm", [P, 2], F32)
        nc.gpsimd.memset(warm[:, 0:1], 0.0)
        nc.scalar.activation(warm[:, 1:2], warm[:, 0:1], ACT.Sigmoid)
        d_byte_table = zeroed_bytes("d_byte_table", G)
        key_bytes = zeroed_bytes("key_bytes", S)

        offs_t = load_list("offs_t", offs)
        x_word_table = load_words("x_word_table", x_words, T)
        for r in four:
            nc.sync.dma_start(x_byte_table[r:P:32, :].bitcast(I32), x_scales[0][r:16:4, :].bitcast(I32))
        w_rows = w1.rearrange("(p j) c -> p j c", j=PACK)
        w_raw = []
        for h in range(2):
            raw = sbuf(f"w_raw{h}", [P, PACK, PACK * HALF], F32)
            nc.sync.dma_start(raw[:], w_rows[:, :, h * PACK * HALF : (h + 1) * PACK * HALF])
            w_raw.append(raw[:].rearrange("p j (m t) -> p m j t", t=PACK))
        n1_t = load_list("n1_t", n1)
        n3_t = load_list("n3_t", n3)
        cand_t = load_list("cand_t", cand)
        n2_t = load_list("n2_t", n2)
        for e in range(2):
            nc.sync.dma_start(d_byte_table[e:P:16, :].bitcast(I32), d_scales[0][e:16:2, :].bitcast(I32))
        k1_t = load_list("k1_t", k1)
        d_word_table = load_words("d_word_table", d_words, G)
        gs_t = load_feature_weights("gs_t", gs)
        gk_t = load_feature_weights("gk_t", gk)
        n4_t = load_list("n4_t", n4)
        n5_t = load_list("n5_t", n5)
        n6_t = load_list("n6_t", n6)

        xq_words = pick("xq_words", x_word_table, offs_t, U32)
        xq_bytes = pick("xq_bytes", x_byte_table, offs_t, U8)
        w_bf = sbuf("w_bf", [P, PACK * S], BF16)
        w_dealt = w_bf[:].rearrange("p (t m j) -> p m j t", t=PACK, j=PACK)
        nc.scalar.copy(w_dealt[:, :HALF], w_raw[0])
        nc.scalar.copy(w_dealt[:, HALF:W_SPLIT], w_raw[1][:, : W_SPLIT - HALF])
        nc.vector.tensor_copy(w_dealt[:, W_SPLIT:], w_raw[1][:, W_SPLIT - HALF :])
        w_words = sbuf("w_words", [P, S], U32)
        w_bytes = sbuf("w_bytes", [P, S], U8)
        y_banks = []
        for t in four:
            cols = slice(t * P, (t + 1) * P)
            nc.vector.quantize_mx(w_words[:, cols].bitcast(FP8X4), w_bytes[:, cols], w_bf[:, t * S : (t + 1) * S])
            y_banks.append(multiply("yb_bank", t, w_words, w_bytes, xq_words, xq_bytes))

        y = four_tiles("y", 2 * S)
        sig1 = four_tiles("sig1_", S)
        for t in four:
            nc.scalar.copy(y[t][:, :S], y_banks[t][:])
            nc.scalar.activation(sig1[t][:], y[t][:].indirect(n1_t[:]), ACT.Sigmoid)

        y3 = four_tiles("y3_", S)
        st = sbuf("st", [P, PACK, S], F32)
        for t in four:
            nc.vector.tensor_copy(y3[t][:], y[t][:].indirect(n3_t[:]))
            nc.vector.tensor_tensor(st[:, t, :], y[t][:, :S], y3[t][:], ALU.subtract)

        gated = four_tiles("gated", S)
        for t in four:
            nc.vector.tensor_tensor(gated[t][:], y[t][:, :S], sig1[t][:], ALU.mult)
        y2 = four_tiles("y2_", S)
        for t in four:
            nc.scalar.activation(y2[t][:], y[t][:].indirect(n2_t[:]), ACT.Copy)

        size = four_tiles("size", S)
        root = four_tiles("root", S)
        for t in four:
            nc.scalar.activation(size[t][:], st[:, t, :], ACT.Abs)
        for t in four:
            nc.scalar.activation(root[t][:], size[t][:], ACT.Abs_reciprocal_sqrt, bias=0.5)

        larger = sbuf("larger", [P, PACK, S], F32)
        for t in four:
            nc.vector.tensor_tensor(larger[:, t, :], gated[t][:], y2[t][:], ALU.max)

        cand_picked_words = pick("cand_picked_words", x_word_table, cand_t, U32)
        cand_picked_bytes = pick("cand_picked_bytes", x_byte_table, cand_t, U8)
        cand_words = deal_words("cand_words", cand_picked_words)
        cand_bytes = deal_bytes("cand_bytes", cand_picked_bytes)

        key_dealt_bytes = deal_bytes("key_dealt_bytes", pick("key_picked_bytes", d_byte_table, k1_t, U8))
        for r in four:
            first = 16 * (r // 2) + r % 2
            nc.sync.dma_start(key_bytes[r:P:32, :].bitcast(I32), key_dealt_bytes[first:P:32, :].bitcast(I32))

        weight = four_tiles("weight", 2 * S)
        weight4 = sbuf("weight4", [P, PACK, S], F32)
        for t in four:
            nc.vector.scalar_tensor_tensor(
                weight[t][:, :S], root[t][:], gk_t[:, t : t + 1], root[t][:], ALU.mult, ALU.mult
            )
            gather(t == PACK - 1, weight4[:, t, :], weight[t], n4_t)

        gs_spread = gs_t[:].unsqueeze(1).unsqueeze(3).to_broadcast([P, S // LINE, PACK, LINE])
        a_banks = score("z", by_lines(larger), gs_spread, cand_words, cand_bytes, "a_bank")
        key_words = deal_words("key_words", pick("key_picked_words", d_word_table, k1_t, U32))
        b_banks = score("z2", by_lines(weight4), by_lines(st), key_words, key_bytes, "yb_bank")

        a = four_tiles("a", S)
        a5 = four_tiles("a5_", W)
        for t in four:
            nc.scalar.activation(a[t][:], a_banks[t][:], ACT.Copy, scale=SCORE_SCALE)
            nc.scalar.activation(a5[t][:], a[t][:].indirect(n5_t[:]), ACT.Copy, scale=-0.5)

        b = four_tiles("b", S)
        b6 = four_tiles("b6_", W)
        out_rows = out.rearrange("(u t e) n -> t u e n", t=PACK, e=RUN)
        for t in four:
            if t == 0:
                nc.vector.tensor_scalar(b[t][:], b_banks[t][:], SCORE_SCALE, None, ALU.mult)
            else:
                nc.scalar.activation(b[t][:], b_banks[t][:], ACT.Copy, scale=SCORE_SCALE)
            gather(t == 0, b6[t][:], b[t], n6_t)
            nc.vector.tensor_tensor(a[t][:].indirect(n5_t[:]), b6[t][:], a5[t][:], ALU.add)
            nc.sync.dma_start(out_rows[t], a[t][:])
